import numpy as np, ml_dtypes
CORES = [16,32,48,64,80]
N = 5
import mx_ref
NC, KT = 512, 3
FROM = [1,4,3,2,0]
BF = ml_dtypes.bfloat16
def setup_inputs(rng):
    def f(*shape):
        return mx_ref.flush((rng.standard_normal(shape, dtype=np.float32) * np.exp2(rng.integers(-2, 3, shape[:-1] + (1,)))).astype(BF))
    return {"w": f(N, 128, KT * 512), "x": f(N, 128, KT * 4 * NC)}
def setup_inputs_blocks(rng):
    d = setup_inputs(rng)
    for k in ("w", "x"): d[k] = mx_ref.spread(d[k], rng, 1)
    return d
def setup_inputs_wide(rng):
    d = setup_inputs(rng)
    for k in ("w", "x"): d[k] = mx_ref.flush((d[k].astype(np.float32) * np.exp2(rng.integers(-8, 9, (N, 1, 1))).astype(np.float32)).astype(BF))
    return d
def setup_inputs_zeros(rng):
    d = setup_inputs(rng); v = d["x"].reshape(N, 128, -1, 4).copy()
    v[np.broadcast_to((rng.random((N, 1, v.shape[2], 1)) < 0.33), v.shape)] = 0
    d["x"] = v.reshape(d["x"].shape)
    return d
def reference(w, x):
    y = np.zeros((N, 128, NC), np.float32)
    for r in range(N):
        for t in range(KT):
            p = mx_ref.matmul(mx_ref.quantize(w[r][:, 512 * t:512 * t + 512]), mx_ref.quantize(x[FROM[r]][:, 4 * NC * t:4 * NC * t + 4 * NC]))
            y[r] = p if t == 0 else y[r] + p
    return {"y": y}

@@ -1,0 +1,161 @@
+from concourse.mybir import dt, ActivationFunctionType
+
+KT, NC, WC = 3, 512, 128
+NSIM = 96
+
+PIECES = [(0, 512), (512, 1024), (1024, 1536)]
+LOADS = [(0, 512, "sync", None), (512, 1024, "scalar", None), (1024, 1536, "sync", None), ("w", 0, "scalar", None)]
+VORDER = [0, 1, 2, "w"]
+ITEMS = [("c", 0, 512, 0), ("c", 512, 1024, 0), ("s", 0, 1024, 0), ("c", 1024, 1536, 0), ("s", 1024, 1536, 0)]
+ROUTES = {}
+TORDER = [0, 1, 2]
+GROUPS = [0, 256, 512]
+
+SCRATCH = {
+    "xb": ("sbuf", [128, 4 * KT * NC], "bfloat16"),
+    "wb": ("sbuf", [128, 4 * KT * WC], "bfloat16"),
+    "xq": ("sbuf", [128, KT * NC], "float8_e4m3fn_x4"),
+    "xs": ("sbuf", [128, KT * NC], "uint8"),
+    "rq": ("sbuf", [128, KT * NC], "float8_e4m3fn_x4"),
+    "rs": ("sbuf", [128, KT * NC], "uint8"),
+    "wq": ("sbuf", [128, KT * WC], "float8_e4m3fn_x4"),
+    "ws": ("sbuf", [128, KT * WC], "uint8"),
+    "acc": ("psum", [128, 512 * (len(GROUPS) - 1)], "float32"),
+    "yb": ("sbuf", [128, NC], "float32"),
+}
+SEMAPHORES = (["ld%d" % i for i in range(len(LOADS))] + ["q%d" % p for p in range(len(PIECES))] + ["qw", "sent"]
+              + ["a%d" % j for j in range(len(ITEMS))]
+              + ["mm%d" % k for k in range(len(GROUPS) - 1)] + ["ev%d" % k for k in range(len(GROUPS) - 1)]
+              + ["st%d" % k for k in range(len(GROUPS) - 1)])
+
+
+def _bits(m):
+    return bin(m).count("1")
+
+
+def _helper(topo, cores, s, d, route):
+    where, idx, _ = ROUTES[route]
+    cand = [c for c in range(NSIM)
+            if topo.chip(c) == topo.chip(s) and c not in cores and topo.may_write(c, d)
+            and (topo.die(c) != topo.die(s)) == (where == "other")]
+    return cand[idx]
+
+
+def _engines(topo, s, h, d, route):
+    kind = ROUTES[route][2]
+    full = topo.mask(s, h)
+    return full & ~topo.mask(s, d) if kind == "spare" else full
+
+
+def _views(T, src_q, src_s, kind, a, b):
+    if kind == "c":
+        return T.rq[:, a:b].bitcast(dt.uint8), src_q[:, a:b].bitcast(dt.uint8)
+    return T.rs[:, a:b], src_s[:, a:b]
+
+
+def _send(g, T, topo, dst, mask, out_ap, in_ap, sem):
+    rid, pid, _ = topo.addr(dst)
+    g.remote_dma(out_ap=out_ap, in_ap=in_ap, remote_sem=sem, local_sem=T.sem.sent, pid=pid, routing_id=rid,
+                 dma_engine_mask=mask)
+    return _bits(mask)
+
+
+def rank_program(g, core, T, topo):
+    cores = list(T.cores)
+    FROM = T.tables["FROM"]
+    TO = [FROM.index(j) for j in range(len(cores))]
+    rank = T.rank_of(core)
+
+    if rank is None:
+        for j, s in enumerate(cores):
+            d = cores[TO[j]]
+            for route in ROUTES:
+                if _helper(topo, cores, s, d, route) != core:
+                    continue
+                sent = 0
+                for i, (kind, a, b, r) in enumerate(ITEMS):
+                    if r != route:
+                        continue
+                    g.wait_ge(T.sem["a%d" % i], _bits(_engines(topo, s, core, d, route)))
+                    o, src = _views(T, T.rq, T.rs, kind, a, b)
+                    sent += _send(g, T, topo, d, topo.mask(core, d), o, src, T.sem["a%d" % i])
+                g.wait_ge(T.sem.sent, sent)
+        return
+
+    d = cores[TO[rank]]
+    queues = {"sync": g.sync, "scalar": g.scalar}
+
+    for i, (a, b, qn, after) in enumerate(LOADS):
+        q = queues[qn]
+        if after is not None:
+            q.wait_ge(T.sem["q%d" % after], 1)
+        if a == "w":
+            q.dma_start(T.wb[:], T.w[:]).then_inc(T.sem["ld%d" % i], 16)
+        else:
+            q.dma_start(T.xb[:, 4 * a:4 * b], T.x[:, 4 * a:4 * b]).then_inc(T.sem["ld%d" % i], 16)
+
+    waited = set()
+    for p in VORDER:
+        if p == "w":
+            i = [k for k, l in enumerate(LOADS) if l[0] == "w"][0]
+            g.vector.wait_ge(T.sem["ld%d" % i], 16)
+            g.vector.quantize_mx(T.wq[:], T.ws[:], T.wb[:]).then_inc(T.sem.qw, 1)
+            continue
+        a, b = PIECES[p]
+        i = [k for k, l in enumerate(LOADS) if l[0] != "w" and l[0] <= a and b <= l[1]][0]
+        if i not in waited:
+            waited.add(i)
+            g.vector.wait_ge(T.sem["ld%d" % i], 16)
+        g.vector.quantize_mx(T.xq[:, a:b], T.xs[:, a:b], T.xb[:, 4 * a:4 * b]).then_inc(T.sem["q%d" % p], 1)
+
+    sent, ready = 0, set()
+    for i, (kind, a, b, r) in enumerate(ITEMS):
+        for p, (pa, pb) in enumerate(PIECES):
+            if pa < b and a < pb and p not in ready:
+                ready.add(p)
+                g.wait_ge(T.sem["q%d" % p], 1)
+        o, src = _views(T, T.xq, T.xs, kind, a, b)
+        if r == 0:
+            sent += _send(g, T, topo, d, topo.mask(core, d), o, src, T.sem["a%d" % i])
+        else:
+            h = _helper(topo, cores, core, d, r)
+            sent += _send(g, T, topo, h, _engines(topo, core, h, d, r), o, src, T.sem["a%d" % i])
+
+    src_core = cores[FROM[rank]]
+    g.tensor.wait_ge(T.sem.qw, 1)
+    ng = len(GROUPS) - 1
+    done, seen = [0] * ng, set()
+    for p in TORDER:
+        a, b = PIECES[p]
+        for i, (kind, ia, ib, r) in enumerate(ITEMS):
+            if ia < b and a < ib and i not in seen:
+                seen.add(i)
+                last = src_core if r == 0 else _helper(topo, cores, src_core, core, r)
+                g.tensor.wait_ge(T.sem["a%d" % i], _bits(topo.mask(last, core)))
+        t = a // NC
+        for k in range(ng):
+            c0, c1 = NC * t + GROUPS[k], NC * t + GROUPS[k + 1]
+            if a <= c0 and c1 <= b:
+                done[k] += 1
+                mm = g.tensor.matmul_mx(T.acc[:, 512 * k:512 * k + (c1 - c0)], T.wq[:, WC * t:WC * t + WC],
+                                        T.ws[:, WC * t:WC * t + WC], T.rq[:, c0:c1], T.rs[:, c0:c1],
+                                        done[k] == 1, done[k] == KT)
+                if done[k] == KT:
+                    mm.then_inc(T.sem["mm%d" % k], 1)
+
+    for k in range(ng):
+        c0, c1 = GROUPS[k], GROUPS[k + 1]
+        bank = T.acc[:, 512 * k:512 * k + (c1 - c0)]
+        if k % 2 == 0:
+            g.vector.wait_ge(T.sem["mm%d" % k], 1)
+            g.vector.tensor_copy(T.yb[:, c0:c1], bank).then_inc(T.sem["ev%d" % k], 1)
+            q = g.sync
+        else:
+            g.scalar.wait_ge(T.sem["mm%d" % k], 1)
+            g.scalar.activation(T.yb[:, c0:c1], bank, ActivationFunctionType.Copy).then_inc(T.sem["ev%d" % k], 1)
+            q = g.scalar
+        q.wait_ge(T.sem["ev%d" % k], 1)
+        q.dma_start(T.y[:, c0:c1], T.yb[:, c0:c1]).then_inc(T.sem["st%d" % k], 16)
+    for k in range(ng):
+        (g.sync if k % 2 == 0 else g.scalar).wait_ge(T.sem["st%d" % k], 16)
+    g.wait_ge(T.sem.sent, sent)

@@ -3,12 +3,13 @@ from concourse.mybir import dt, ActivationFunctionType
 KT, NC, WC = 3, 512, 128
 NSIM = 96
 
-PIECES = [(0, 512), (512, 1024), (1024, 1536)]
-LOADS = [(0, 512, "sync", None), (512, 1024, "scalar", None), (1024, 1536, "sync", None), ("w", 0, "scalar", None)]
-VORDER = [0, 1, 2, "w"]
-ITEMS = [("c", 0, 512, 0), ("c", 512, 1024, 0), ("s", 0, 1024, 0), ("c", 1024, 1536, 0), ("s", 1024, 1536, 0)]
-ROUTES = {}
-TORDER = [0, 1, 2]
+PIECES = [(0, 256), (256, 512), (512, 768), (768, 1024), (1024, 1536)]
+LOADS = [(0, 256, "sync", None), (256, 512, "scalar", None), (512, 768, "sync", None), (768, 1024, "scalar", None),
+         (1024, 1536, "sync", None), ("w", 0, "scalar", None)]
+VORDER = [0, 1, 2, 3, 4, "w"]
+ITEMS = [("c", 0, 256, 1), ("s", 0, 256, 1), ("c", 256, 512, 2), ("s", 256, 512, 2), ("c", 512, 768, 3),
+         ("s", 512, 768, 3), ("c", 768, 1024, 0), ("s", 768, 1024, 0), ("c", 1024, 1536, 0), ("s", 1024, 1536, 0)]
+ROUTES = {1: ("other", 0, "all"), 2: ("other", 1, "all"), 3: ("other", 2, "all")}
 GROUPS = [0, 256, 512]
 
 SCRATCH = {
@@ -124,24 +125,20 @@ def rank_program(g, core, T, topo):
     src_core = cores[FROM[rank]]
     g.tensor.wait_ge(T.sem.qw, 1)
     ng = len(GROUPS) - 1
-    done, seen = [0] * ng, set()
-    for p in TORDER:
-        a, b = PIECES[p]
-        for i, (kind, ia, ib, r) in enumerate(ITEMS):
-            if ia < b and a < ib and i not in seen:
-                seen.add(i)
-                last = src_core if r == 0 else _helper(topo, cores, src_core, core, r)
-                g.tensor.wait_ge(T.sem["a%d" % i], _bits(topo.mask(last, core)))
-        t = a // NC
+    seen = set()
+    for t in range(KT):
         for k in range(ng):
             c0, c1 = NC * t + GROUPS[k], NC * t + GROUPS[k + 1]
-            if a <= c0 and c1 <= b:
-                done[k] += 1
-                mm = g.tensor.matmul_mx(T.acc[:, 512 * k:512 * k + (c1 - c0)], T.wq[:, WC * t:WC * t + WC],
-                                        T.ws[:, WC * t:WC * t + WC], T.rq[:, c0:c1], T.rs[:, c0:c1],
-                                        done[k] == 1, done[k] == KT)
-                if done[k] == KT:
-                    mm.then_inc(T.sem["mm%d" % k], 1)
+            for i, (kind, ia, ib, r) in enumerate(ITEMS):
+                if ia < c1 and c0 < ib and i not in seen:
+                    seen.add(i)
+                    last = src_core if r == 0 else _helper(topo, cores, src_core, core, r)
+                    g.tensor.wait_ge(T.sem["a%d" % i], _bits(topo.mask(last, core)))
+            mm = g.tensor.matmul_mx(T.acc[:, 512 * k:512 * k + (c1 - c0)], T.wq[:, WC * t:WC * t + WC],
+                                    T.ws[:, WC * t:WC * t + WC], T.rq[:, c0:c1], T.rs[:, c0:c1],
+                                    t == 0, t == KT - 1)
+            if t == KT - 1:
+                mm.then_inc(T.sem["mm%d" % k], 1)
 
     for k in range(ng):
         c0, c1 = GROUPS[k], GROUPS[k + 1]

@@ -4,14 +4,16 @@ KT, NC, WC = 3, 512, 128
 NSIM = 96
 
 PIECES = [(0, 256), (256, 512), (512, 768), (768, 1024), (1024, 1536)]
-LOADS = [(0, 256, "sync", None), (256, 512, "scalar", None), (512, 768, "sync", None), (768, 1024, "scalar", None),
-         (1024, 1536, "sync", None), ("w", 0, "scalar", None)]
+LOADS = [(0, 256, "sync"), (256, 512, "scalar"), (512, 768, "sync"), (768, 1024, "scalar"),
+         (1024, 1536, "sync"), ("w", 0, "scalar")]
 VORDER = [0, 1, 2, 3, 4, "w"]
-ITEMS = [("c", 0, 256, 1), ("s", 0, 256, 1), ("c", 256, 512, 2), ("s", 256, 512, 2), ("c", 512, 768, 3),
-         ("s", 512, 768, 3), ("c", 768, 1024, 0), ("s", 768, 1024, 0), ("c", 1024, 1536, 0), ("s", 1024, 1536, 0)]
-ROUTES = {1: ("other", 0, "all"), 2: ("other", 1, "all"), 3: ("other", 2, "all")}
-GROUPS = [0, 256, 512]
+ITEMS = [("c", 0, 256, 1), ("s", 0, 512, 4), ("c", 256, 512, 2), ("c", 512, 768, 3),
+         ("s", 512, 1536, 0), ("c", 768, 1408, 0), ("c", 1408, 1536, 0)]
+ROUTES = {1: 0, 2: 1, 3: 2, 4: 3}
+GROUPS = [0, 256, 384, 512]
+MMORD = [(0, 0), (0, 1), (0, 2), (1, 1), (1, 2), (2, 0), (2, 1), (1, 0), (2, 2)]
 
+NG = len(GROUPS) - 1
 SCRATCH = {
     "xb": ("sbuf", [128, 4 * KT * NC], "bfloat16"),
     "wb": ("sbuf", [128, 4 * KT * WC], "bfloat16"),
@@ -21,13 +23,12 @@ SCRATCH = {
     "rs": ("sbuf", [128, KT * NC], "uint8"),
     "wq": ("sbuf", [128, KT * WC], "float8_e4m3fn_x4"),
     "ws": ("sbuf", [128, KT * WC], "uint8"),
-    "acc": ("psum", [128, 512 * (len(GROUPS) - 1)], "float32"),
+    "acc": ("psum", [128, 512 * NG], "float32"),
     "yb": ("sbuf", [128, NC], "float32"),
 }
-SEMAPHORES = (["ld%d" % i for i in range(len(LOADS))] + ["q%d" % p for p in range(len(PIECES))] + ["qw", "sent"]
+SEMAPHORES = (["ld%d" % i for i in range(len(LOADS))] + ["q%d" % p for p in range(len(PIECES))] + ["qw", "sent", "go"]
               + ["a%d" % j for j in range(len(ITEMS))]
-              + ["mm%d" % k for k in range(len(GROUPS) - 1)] + ["ev%d" % k for k in range(len(GROUPS) - 1)]
-              + ["st%d" % k for k in range(len(GROUPS) - 1)])
+              + ["mm%d" % k for k in range(NG)] + ["ev%d" % k for k in range(NG)] + ["st%d" % k for k in range(NG)])
 
 
 def _bits(m):
@@ -35,17 +36,10 @@ def _bits(m):
 
 
 def _helper(topo, cores, s, d, route):
-    where, idx, _ = ROUTES[route]
     cand = [c for c in range(NSIM)
             if topo.chip(c) == topo.chip(s) and c not in cores and topo.may_write(c, d)
-            and (topo.die(c) != topo.die(s)) == (where == "other")]
-    return cand[idx]
-
-
-def _engines(topo, s, h, d, route):
-    kind = ROUTES[route][2]
-    full = topo.mask(s, h)
-    return full & ~topo.mask(s, d) if kind == "spare" else full
+            and topo.die(c) != topo.die(s)]
+    return cand[ROUTES[route]]
 
 
 def _views(T, src_q, src_s, kind, a, b):
@@ -54,8 +48,9 @@ def _views(T, src_q, src_s, kind, a, b):
     return T.rs[:, a:b], src_s[:, a:b]
 
 
-def _send(g, T, topo, dst, mask, out_ap, in_ap, sem):
+def _send(g, T, topo, src, dst, out_ap, in_ap, sem):
     rid, pid, _ = topo.addr(dst)
+    mask = topo.mask(src, dst)
     g.remote_dma(out_ap=out_ap, in_ap=in_ap, remote_sem=sem, local_sem=T.sem.sent, pid=pid, routing_id=rid,
                  dma_engine_mask=mask)
     return _bits(mask)
@@ -77,25 +72,22 @@ def rank_program(g, core, T, topo):
                 for i, (kind, a, b, r) in enumerate(ITEMS):
                     if r != route:
                         continue
-                    g.wait_ge(T.sem["a%d" % i], _bits(_engines(topo, s, core, d, route)))
+                    g.wait_ge(T.sem["a%d" % i], _bits(topo.mask(s, core)))
                     o, src = _views(T, T.rq, T.rs, kind, a, b)
-                    sent += _send(g, T, topo, d, topo.mask(core, d), o, src, T.sem["a%d" % i])
+                    sent += _send(g, T, topo, core, d, o, src, T.sem["a%d" % i])
                 g.wait_ge(T.sem.sent, sent)
         return
 
     d = cores[TO[rank]]
     queues = {"sync": g.sync, "scalar": g.scalar}
 
-    for i, (a, b, qn, after) in enumerate(LOADS):
-        q = queues[qn]
-        if after is not None:
-            q.wait_ge(T.sem["q%d" % after], 1)
+    for i, (a, b, qn) in enumerate(LOADS):
         if a == "w":
-            q.dma_start(T.wb[:], T.w[:]).then_inc(T.sem["ld%d" % i], 16)
+            queues[qn].wait_ge(T.sem.go, 1)
+            queues[qn].dma_start(T.wb[:], T.w[:]).then_inc(T.sem["ld%d" % i], 16)
         else:
-            q.dma_start(T.xb[:, 4 * a:4 * b], T.x[:, 4 * a:4 * b]).then_inc(T.sem["ld%d" % i], 16)
+            queues[qn].dma_start(T.xb[:, 4 * a:4 * b], T.x[:, 4 * a:4 * b]).then_inc(T.sem["ld%d" % i], 16)
 
-    waited = set()
     for p in VORDER:
         if p == "w":
             i = [k for k, l in enumerate(LOADS) if l[0] == "w"][0]
@@ -103,47 +95,44 @@ def rank_program(g, core, T, topo):
             g.vector.quantize_mx(T.wq[:], T.ws[:], T.wb[:]).then_inc(T.sem.qw, 1)
             continue
         a, b = PIECES[p]
-        i = [k for k, l in enumerate(LOADS) if l[0] != "w" and l[0] <= a and b <= l[1]][0]
-        if i not in waited:
-            waited.add(i)
-            g.vector.wait_ge(T.sem["ld%d" % i], 16)
+        i = [k for k, l in enumerate(LOADS) if l[0] == a and l[1] == b][0]
+        g.vector.wait_ge(T.sem["ld%d" % i], 16)
         g.vector.quantize_mx(T.xq[:, a:b], T.xs[:, a:b], T.xb[:, 4 * a:4 * b]).then_inc(T.sem["q%d" % p], 1)
 
     sent, ready = 0, set()
+    last_relayed = max(i for i, it in enumerate(ITEMS) if it[3] != 0)
     for i, (kind, a, b, r) in enumerate(ITEMS):
         for p, (pa, pb) in enumerate(PIECES):
             if pa < b and a < pb and p not in ready:
                 ready.add(p)
                 g.wait_ge(T.sem["q%d" % p], 1)
         o, src = _views(T, T.xq, T.xs, kind, a, b)
-        if r == 0:
-            sent += _send(g, T, topo, d, topo.mask(core, d), o, src, T.sem["a%d" % i])
-        else:
-            h = _helper(topo, cores, core, d, r)
-            sent += _send(g, T, topo, h, _engines(topo, core, h, d, r), o, src, T.sem["a%d" % i])
+        sent += _send(g, T, topo, core, d if r == 0 else _helper(topo, cores, core, d, r), o, src, T.sem["a%d" % i])
+        if i == last_relayed:
+            g.sem_inc(T.sem.go, 1)
 
     src_core = cores[FROM[rank]]
     g.tensor.wait_ge(T.sem.qw, 1)
-    ng = len(GROUPS) - 1
-    seen = set()
-    for t in range(KT):
-        for k in range(ng):
-            c0, c1 = NC * t + GROUPS[k], NC * t + GROUPS[k + 1]
-            for i, (kind, ia, ib, r) in enumerate(ITEMS):
-                if ia < c1 and c0 < ib and i not in seen:
-                    seen.add(i)
-                    last = src_core if r == 0 else _helper(topo, cores, src_core, core, r)
-                    g.tensor.wait_ge(T.sem["a%d" % i], _bits(topo.mask(last, core)))
-            mm = g.tensor.matmul_mx(T.acc[:, 512 * k:512 * k + (c1 - c0)], T.wq[:, WC * t:WC * t + WC],
-                                    T.ws[:, WC * t:WC * t + WC], T.rq[:, c0:c1], T.rs[:, c0:c1],
-                                    t == 0, t == KT - 1)
-            if t == KT - 1:
-                mm.then_inc(T.sem["mm%d" % k], 1)
+    seen, done = set(), [0] * NG
+    for t, k in MMORD:
+        c0, c1 = NC * t + GROUPS[k], NC * t + GROUPS[k + 1]
+        for i, (kind, ia, ib, r) in enumerate(ITEMS):
+            if ia < c1 and c0 < ib and i not in seen:
+                seen.add(i)
+                last = src_core if r == 0 else _helper(topo, cores, src_core, core, r)
+                g.tensor.wait_ge(T.sem["a%d" % i], _bits(topo.mask(last, core)))
+        done[k] += 1
+        mm = g.tensor.matmul_mx(T.acc[:, 512 * k:512 * k + (c1 - c0)], T.wq[:, WC * t:WC * t + WC],
+                                T.ws[:, WC * t:WC * t + WC], T.rq[:, c0:c1], T.rs[:, c0:c1],
+                                done[k] == 1, done[k] == KT)
+        if done[k] == KT:
+            mm.then_inc(T.sem["mm%d" % k], 1)
 
-    for k in range(ng):
+    order = [k for n, (t, k) in enumerate(MMORD) if k not in [kk for _, kk in MMORD[n + 1:]]]
+    for n, k in enumerate(order):
         c0, c1 = GROUPS[k], GROUPS[k + 1]
         bank = T.acc[:, 512 * k:512 * k + (c1 - c0)]
-        if k % 2 == 0:
+        if n % 2 == 1:
             g.vector.wait_ge(T.sem["mm%d" % k], 1)
             g.vector.tensor_copy(T.yb[:, c0:c1], bank).then_inc(T.sem["ev%d" % k], 1)
             q = g.sync
@@ -153,6 +142,6 @@ def rank_program(g, core, T, topo):
             q = g.scalar
         q.wait_ge(T.sem["ev%d" % k], 1)
         q.dma_start(T.y[:, c0:c1], T.yb[:, c0:c1]).then_inc(T.sem["st%d" % k], 16)
-    for k in range(ng):
-        (g.sync if k % 2 == 0 else g.scalar).wait_ge(T.sem["st%d" % k], 16)
+    for n, k in enumerate(order):
+        (g.sync if n % 2 == 1 else g.scalar).wait_ge(T.sem["st%d" % k], 16)
     g.wait_ge(T.sem.sent, sent)

from concourse.mybir import dt, ActivationFunctionType

KT, NC, WC = 3, 512, 128
NSIM = 96

PIECES = [(0, 256), (256, 512), (512, 768), (768, 1024), (1024, 1536)]
LOADS = [(0, 256, "sync"), (256, 512, "scalar"), (512, 768, "sync"), (768, 1024, "scalar"),
         (1024, 1536, "sync"), ("w", 0, "scalar")]
VORDER = [0, 1, 2, 3, 4, "w"]
ITEMS = [("c", 0, 256, 1), ("s", 0, 512, 4), ("c", 256, 512, 2), ("c", 512, 768, 3),
         ("s", 512, 1536, 0), ("c", 768, 1408, 0), ("c", 1408, 1536, 0)]
ROUTES = {1: 0, 2: 1, 3: 2, 4: 3}
GROUPS = [0, 256, 384, 512]
MMORD = [(0, 0), (0, 1), (0, 2), (1, 1), (1, 2), (2, 0), (2, 1), (1, 0), (2, 2)]

NG = len(GROUPS) - 1
SCRATCH = {
    "xb": ("sbuf", [128, 4 * KT * NC], "bfloat16"),
    "wb": ("sbuf", [128, 4 * KT * WC], "bfloat16"),
    "xq": ("sbuf", [128, KT * NC], "float8_e4m3fn_x4"),
    "xs": ("sbuf", [128, KT * NC], "uint8"),
    "rq": ("sbuf", [128, KT * NC], "float8_e4m3fn_x4"),
    "rs": ("sbuf", [128, KT * NC], "uint8"),
    "wq": ("sbuf", [128, KT * WC], "float8_e4m3fn_x4"),
    "ws": ("sbuf", [128, KT * WC], "uint8"),
    "acc": ("psum", [128, 512 * NG], "float32"),
    "yb": ("sbuf", [128, NC], "float32"),
}
SEMAPHORES = (["ld%d" % i for i in range(len(LOADS))] + ["q%d" % p for p in range(len(PIECES))] + ["qw", "sent", "go"]
              + ["a%d" % j for j in range(len(ITEMS))]
              + ["mm%d" % k for k in range(NG)] + ["ev%d" % k for k in range(NG)] + ["st%d" % k for k in range(NG)])


def _bits(m):
    return bin(m).count("1")


def _helper(topo, cores, s, d, route):
    cand = [c for c in range(NSIM)
            if topo.chip(c) == topo.chip(s) and c not in cores and topo.may_write(c, d)
            and topo.die(c) != topo.die(s)]
    return cand[ROUTES[route]]


def _views(T, src_q, src_s, kind, a, b):
    if kind == "c":
        return T.rq[:, a:b].bitcast(dt.uint8), src_q[:, a:b].bitcast(dt.uint8)
    return T.rs[:, a:b], src_s[:, a:b]


def _send(g, T, topo, src, dst, out_ap, in_ap, sem):
    rid, pid, _ = topo.addr(dst)
    mask = topo.mask(src, dst)
    g.remote_dma(out_ap=out_ap, in_ap=in_ap, remote_sem=sem, local_sem=T.sem.sent, pid=pid, routing_id=rid,
                 dma_engine_mask=mask)
    return _bits(mask)


def rank_program(g, core, T, topo):
    cores = list(T.cores)
    FROM = T.tables["FROM"]
    TO = [FROM.index(j) for j in range(len(cores))]
    rank = T.rank_of(core)

    if rank is None:
        for j, s in enumerate(cores):
            d = cores[TO[j]]
            for route in ROUTES:
                if _helper(topo, cores, s, d, route) != core:
                    continue
                sent = 0
                for i, (kind, a, b, r) in enumerate(ITEMS):
                    if r != route:
                        continue
                    g.wait_ge(T.sem["a%d" % i], _bits(topo.mask(s, core)))
                    o, src = _views(T, T.rq, T.rs, kind, a, b)
                    sent += _send(g, T, topo, core, d, o, src, T.sem["a%d" % i])
                g.wait_ge(T.sem.sent, sent)
        return

    d = cores[TO[rank]]
    queues = {"sync": g.sync, "scalar": g.scalar}

    for i, (a, b, qn) in enumerate(LOADS):
        if a == "w":
            queues[qn].wait_ge(T.sem.go, 1)
            queues[qn].dma_start(T.wb[:], T.w[:]).then_inc(T.sem["ld%d" % i], 16)
        else:
            queues[qn].dma_start(T.xb[:, 4 * a:4 * b], T.x[:, 4 * a:4 * b]).then_inc(T.sem["ld%d" % i], 16)

    for p in VORDER:
        if p == "w":
            i = [k for k, l in enumerate(LOADS) if l[0] == "w"][0]
            g.vector.wait_ge(T.sem["ld%d" % i], 16)
            g.vector.quantize_mx(T.wq[:], T.ws[:], T.wb[:]).then_inc(T.sem.qw, 1)
            continue
        a, b = PIECES[p]
        i = [k for k, l in enumerate(LOADS) if l[0] == a and l[1] == b][0]
        g.vector.wait_ge(T.sem["ld%d" % i], 16)
        g.vector.quantize_mx(T.xq[:, a:b], T.xs[:, a:b], T.xb[:, 4 * a:4 * b]).then_inc(T.sem["q%d" % p], 1)

    sent, ready = 0, set()
    last_relayed = max(i for i, it in enumerate(ITEMS) if it[3] != 0)
    for i, (kind, a, b, r) in enumerate(ITEMS):
        for p, (pa, pb) in enumerate(PIECES):
            if pa < b and a < pb and p not in ready:
                ready.add(p)
                g.wait_ge(T.sem["q%d" % p], 1)
        o, src = _views(T, T.xq, T.xs, kind, a, b)
        sent += _send(g, T, topo, core, d if r == 0 else _helper(topo, cores, core, d, r), o, src, T.sem["a%d" % i])
        if i == last_relayed:
            g.sem_inc(T.sem.go, 1)

    src_core = cores[FROM[rank]]
    g.tensor.wait_ge(T.sem.qw, 1)
    seen, done = set(), [0] * NG
    for t, k in MMORD:
        c0, c1 = NC * t + GROUPS[k], NC * t + GROUPS[k + 1]
        for i, (kind, ia, ib, r) in enumerate(ITEMS):
            if ia < c1 and c0 < ib and i not in seen:
                seen.add(i)
                last = src_core if r == 0 else _helper(topo, cores, src_core, core, r)
                g.tensor.wait_ge(T.sem["a%d" % i], _bits(topo.mask(last, core)))
        done[k] += 1
        mm = g.tensor.matmul_mx(T.acc[:, 512 * k:512 * k + (c1 - c0)], T.wq[:, WC * t:WC * t + WC],
                                T.ws[:, WC * t:WC * t + WC], T.rq[:, c0:c1], T.rs[:, c0:c1],
                                done[k] == 1, done[k] == KT)
        if done[k] == KT:
            mm.then_inc(T.sem["mm%d" % k], 1)

    order = [k for n, (t, k) in enumerate(MMORD) if k not in [kk for _, kk in MMORD[n + 1:]]]
    for n, k in enumerate(order):
        c0, c1 = GROUPS[k], GROUPS[k + 1]
        bank = T.acc[:, 512 * k:512 * k + (c1 - c0)]
        if n % 2 == 1:
            g.vector.wait_ge(T.sem["mm%d" % k], 1)
            g.vector.tensor_copy(T.yb[:, c0:c1], bank).then_inc(T.sem["ev%d" % k], 1)
            q = g.sync
        else:
            g.scalar.wait_ge(T.sem["mm%d" % k], 1)
            g.scalar.activation(T.yb[:, c0:c1], bank, ActivationFunctionType.Copy).then_inc(T.sem["ev%d" % k], 1)
            q = g.scalar
        q.wait_ge(T.sem["ev%d" % k], 1)
        q.dma_start(T.y[:, c0:c1], T.yb[:, c0:c1]).then_inc(T.sem["st%d" % k], 16)
    for n, k in enumerate(order):
        (g.sync if n % 2 == 1 else g.scalar).wait_ge(T.sem["st%d" % k], 16)
    g.wait_ge(T.sem.sent, sent)
